import numpy as np
import ml_dtypes


def mxq(x, axis, fmt="e4m3"):
    dtype, down = {"e4m3": (ml_dtypes.float8_e4m3fn, 7), "e5m2": (ml_dtypes.float8_e5m2, 14)}[fmt]
    v = np.moveaxis(np.asarray(x, np.float32).astype(ml_dtypes.bfloat16).astype(np.float64), axis, -1)
    blocks = v.reshape(v.shape[:-1] + (-1, 32))
    amax = np.abs(blocks).max(-1, keepdims=True)
    byte = np.maximum(np.where(amax > 0, np.frexp(amax)[1] - 1 + 127, 0) - down, 1)
    scale = np.exp2(byte - 127.0)
    codes = (blocks / scale).astype(np.float32).astype(dtype).astype(np.float64)
    return np.moveaxis((codes * scale).reshape(v.shape), -1, axis)


WIDE = False


def mx_kscale(k):
    if not WIDE:
        return np.ones(k)
    levels = np.array([10, -10, 5, -5, 0])
    if k % 512:
        return np.exp2(np.random.permutation(np.resize(levels, k // 32))).repeat(32)
    a = np.empty((k // 512, 16))
    for p in range(k // 512):
        a[p, :8] = np.random.permutation(np.resize(levels, 8))
        for g in range(8):
            far = levels[np.abs(levels - a[p, g]) >= 10]
            a[p, g + 8] = far[np.random.randint(len(far))]
    return np.exp2(a.ravel()).repeat(32)


def f64(x):
    return np.asarray(x).astype(np.float64)


def striped8(idx):
    return np.asarray(idx).reshape(8, -1, 16).transpose(0, 2, 1).reshape(128, -1).astype(np.uint16)


def unstriped8(offs):
    return offs.reshape(8, 16, -1).transpose(0, 2, 1).reshape(8, -1).astype(np.int64)


def pick8(x, idx, run):
    r = np.arange(len(x))
    return x[r[:, None], idx[r % (8 * run) // run]]


E2M1 = np.array([0.0, 0.5, 1.0, 1.5, 2.0, 3.0, 4.0, 6.0, -0.0, -0.5, -1.0, -1.5, -2.0, -3.0, -4.0, -6.0])


def pack_weight(w, fmt):
    k, n = w.shape
    w = f64(np.asarray(w, np.float32).astype(ml_dtypes.bfloat16)).reshape(k // 32, 32, n)
    amax = np.abs(w).max(1)
    if fmt == "e4m3":
        byte = np.frexp(amax)[1] - 1 + 127 - 7
    else:
        mant, ex = np.frexp(amax / 6.0)
        byte = np.where(mant > 0.5, ex, ex - 1) + 127
    byte = np.clip(np.where(amax > 0, byte, 1), 1, 254)
    scaled = (w * np.exp2(127.0 - byte)[:, None, :]).reshape(k, n).astype(np.float32)
    by_word = np.ascontiguousarray(scaled.reshape(k // 512, 128, 4, n).transpose(0, 1, 3, 2))
    if fmt == "e4m3":
        words = by_word.astype(ml_dtypes.float8_e4m3fn).view(np.uint8)
    else:
        c = by_word.astype(ml_dtypes.float4_e2m1fn).view(np.uint8) & 0xF
        words = (c[..., 0::2] | (c[..., 1::2] << 4)).reshape(k // 512, 128, 2 * n)
    return np.ascontiguousarray(words), np.ascontiguousarray(byte.astype(np.uint8).reshape(k // 512, 16, n))


def unpack_weight(words, scales, fmt):
    g, _, n = scales.shape
    words = np.ascontiguousarray(words).reshape(g, 128, n, -1)
    if fmt == "e4m3":
        vals = words.view(ml_dtypes.float8_e4m3fn).astype(np.float64)
    else:
        nib = np.empty((g, 128, n, 4), np.uint8)
        nib[..., 0::2] = words & 0xF
        nib[..., 1::2] = words >> 4
        vals = E2M1[nib]
    vals = vals * np.repeat(np.exp2(scales.astype(np.float64) - 127.0), 8, axis=1)[..., None]
    return vals.transpose(0, 1, 3, 2).reshape(g * 512, n)


D, E, T, Q, I = 512, 512, 1024, 128, 512


def setup_inputs():
    n = np.random.standard_normal
    idx = np.stack([np.random.permutation(T)[:I] for _ in range(8)])
    idx2 = np.stack([np.random.permutation(T)[:I] for _ in range(8)])
    fd = mx_kscale(D)
    fe = mx_kscale(E)
    keysp = pack_weight(n((D, T)) / fd[:, None], "e4m3")
    return {
        "query": (n((D, Q)) * 0.7 / np.sqrt(D) * fd[:, None]).astype(np.float32),
        "keys_words": keysp[0],
        "keys_scales": keysp[1],
        "gout": (n((E, Q)) * 1 / np.sqrt(E) * fe[:, None]).astype(np.float32),
        "vals": (n((E, T)) / fe[:, None]).astype(np.float32),
        "old": (0.5 * n((Q, T))).astype(np.float32),
        "offs": striped8(idx),
        "offs2": striped8(idx2),
    }


def reference(query, keys_words, keys_scales, gout, vals, old, offs, offs2):
    idx = unstriped8(offs)
    idx2 = unstriped8(offs2)
    keysu = unpack_weight(keys_words, keys_scales, "e4m3")
    queryq = mxq(f64(query), 0, "e4m3")
    a = queryq.T @ keysu
    s = pick8(a, idx, 16) * pick8(a, idx2, 16) + (pick8(a, idx, 16) + pick8(a, idx2, 16)) * 0.5
    p = np.exp(s - np.max(s, axis=1, keepdims=True))
    z = np.sum(p, axis=1, keepdims=True)
    goutq = mxq(f64(gout), 0, "e4m3")
    valsq = mxq(f64(vals), 0, "e4m3")
    c0 = goutq.T @ valsq
    dw = pick8(c0, idx, 16)
    dz = np.sum(dw * p / np.square(z) * (-1.0), axis=1, keepdims=True)
    dp = dw / z + dz
    ds = dp * p
    e1 = ds * pick8(a, idx2, 16)
    s1 = np.zeros((Q, T))
    s1[np.arange(Q)[:, None], idx[np.arange(Q) % 128 // 16]] = e1
    e2 = ds * 0.5
    s2 = np.zeros((Q, T))
    s2[np.arange(Q)[:, None], idx[np.arange(Q) % 128 // 16]] = e2
    e3 = ds * pick8(a, idx, 16)
    s3 = np.zeros((Q, T))
    s3[np.arange(Q)[:, None], idx2[np.arange(Q) % 128 // 16]] = e3
    e4 = ds * 0.5
    s4 = np.zeros((Q, T))
    s4[np.arange(Q)[:, None], idx2[np.arange(Q) % 128 // 16]] = e4
    da = s1 + s2 + s3 + s4
    y = da * 512.0 + f64(old)
    return y

@@ -1,0 +1,190 @@
+from contextlib import ExitStack
+
+import concourse.mybir as mybir
+from concourse.masks import make_identity
+
+D, E, T, Q, SLOTS = 512, 512, 1024, 128, 512
+FLOPS = 2 * Q * T * (D + E)
+
+F32 = mybir.dt.float32
+BF16 = mybir.dt.bfloat16
+I32 = mybir.dt.int32
+U32 = mybir.dt.uint32
+U16 = mybir.dt.uint16
+U8 = mybir.dt.uint8
+FP8X4 = mybir.dt.float8_e4m3fn_x4
+ALU = mybir.AluOpType
+ACT = mybir.ActivationFunctionType
+
+P = 128
+PACK = 4
+BANK = 512
+CHUNKS = (256, 256, 256, 256)
+STARTS = (0, 256, 512, 768)
+SCALAR_SHARE = (256, 256, 160, 96)
+OUT_SCALE = 512.0
+PIECES = 4
+A_PARTS = 4
+
+
+def interleave(copy, grouped, raw, c0, c1):
+    copy(
+        grouped[:, c0:c1, :].rearrange("p (c i) t -> p c t i", i=4),
+        raw[:, :, c0:c1].rearrange("p t (c i) -> p c t i", i=4),
+    )
+
+
+def tile_attend_bproductpairs_heads_kernel(tc, query, keys_words, keys_scales, gout, vals, old, offs, offs2, out):
+    nc = tc.nc
+    with ExitStack() as ctx:
+        sb = ctx.enter_context(tc.tile_pool(name="sb", bufs=1))
+        ps = ctx.enter_context(tc.psum_pool(name="ps", bufs=1))
+
+        first = sb.tile([P, SLOTS // 16], U16, name="first")
+        second = sb.tile([P, SLOTS // 16], U16, name="second")
+        k_codes = [sb.tile([P, BANK], U32, name=f"k_codes{h}", align_bytes=64) for h in range(2)]
+        k_scales = sb.tile([P, T], U8, name="k_scales", align_bytes=64)
+        q_raw = sb.tile([P, PACK, Q], F32, name="q_raw")
+        g_raw = sb.tile([P, PACK, Q], F32, name="g_raw")
+        v_raw = [sb.tile([P, PACK, width], F32, name=f"v_raw{c}") for c, width in enumerate(CHUNKS)]
+        old_sb = sb.tile([P, T], F32, name="old_sb")
+
+        nc.gpsimd.memset(k_scales[:].bitcast(I32), 0)
+        words = keys_words[0].rearrange("p n t -> p (n t)").bitcast(I32)
+        vals_k = vals.rearrange("(p j) w -> p j w", j=PACK)
+        nc.sync.dma_start(out=q_raw[:], in_=query.rearrange("(p j) w -> p j w", j=PACK))
+        nc.sync.dma_start(out=k_codes[0][:].bitcast(I32), in_=words[:, :BANK])
+        for quad in range(4):
+            nc.sync.dma_start(
+                out=k_scales[32 * quad : 32 * quad + 4, :].bitcast(I32),
+                in_=keys_scales[0, 4 * quad : 4 * quad + 4, :].bitcast(I32),
+            )
+        nc.sync.dma_start(out=k_codes[1][:].bitcast(I32), in_=words[:, BANK:])
+        nc.sync.dma_start(out=g_raw[:], in_=gout.rearrange("(p j) w -> p j w", j=PACK))
+        nc.sync.dma_start(first[:], offs)
+        nc.sync.dma_start(second[:], offs2)
+        nc.sync.dma_start(out=v_raw[0][:], in_=vals_k[:, :, STARTS[0] : STARTS[0] + CHUNKS[0]])
+        nc.sync.dma_start(out=v_raw[1][:], in_=vals_k[:, :, STARTS[1] : STARTS[1] + CHUNKS[1]])
+        nc.sync.dma_start(out=v_raw[2][:], in_=vals_k[:, :, STARTS[2] : STARTS[2] + CHUNKS[2]])
+        nc.sync.dma_start(out=v_raw[3][:], in_=vals_k[:, :, STARTS[3] : STARTS[3] + CHUNKS[3]])
+        nc.sync.dma_start(out=old_sb[:], in_=old)
+
+
+        consts = sb.tile([P, 2], F32, name="consts")
+        nc.vector.memset(consts[:, 0:1], OUT_SCALE)
+        nc.vector.memset(consts[:, 1:2], 0.5 * OUT_SCALE)
+        by_first = sb.tile([P, T], F32, name="by_first")
+        by_second = sb.tile([P, T], F32, name="by_second")
+        nc.vector.memset(by_first[:], 0.0)
+        nc.vector.memset(by_second[:], 0.0)
+        ident = sb.tile([P, P], F32, name="ident")
+        make_identity(nc, ident[:])
+
+        def quantize(grouped, name, width):
+            codes = sb.tile([P, width], U32, name=name + "_codes", align_bytes=64)
+            scales = sb.tile([P, width], U8, name=name + "_scales", align_bytes=64)
+            nc.vector.quantize_mx(out=codes[:].bitcast(FP8X4), scales=scales[:], in_=grouped[:].rearrange("p w j -> p (w j)"))
+            return codes, scales
+
+        q_grouped = sb.tile([P, Q, PACK], BF16, name="q_grouped", align_bytes=64)
+        interleave(nc.vector.tensor_copy, q_grouped, q_raw, 0, Q)
+        q_codes, q_scales = quantize(q_grouped, "q", Q)
+
+        a_sb = sb.tile([P, T], F32, name="a_sb")
+        a_width = T // A_PARTS
+        for part in range(A_PARTS):
+            col = part * a_width
+            acc = ps.tile([P, BANK], F32, name=f"a_bank{part}")
+            nc.tensor.matmul_mx(
+                out=acc[:, :a_width], lhsT=q_codes[:].bitcast(FP8X4), lhsT_scale=q_scales[:],
+                rhs=k_codes[col // BANK][:, col % BANK : col % BANK + a_width].bitcast(FP8X4),
+                rhs_scale=k_scales[:, col : col + a_width], start=True, stop=True,
+            )
+            if part % 2 == 0:
+                nc.scalar.activation(a_sb[:, col : col + a_width], acc[:, :a_width], ACT.Copy)
+            else:
+                nc.vector.tensor_copy(a_sb[:, col : col + a_width], acc[:, :a_width])
+
+        g_grouped = sb.tile([P, Q, PACK], BF16, name="g_grouped", align_bytes=64)
+        interleave(nc.vector.tensor_copy, g_grouped, g_raw, 0, Q)
+        g_codes, g_scales = quantize(g_grouped, "g", Q)
+
+        u1 = sb.tile([P, SLOTS], F32, name="u1")
+        a2 = sb.tile([P, SLOTS], F32, name="a2")
+        nc.vector.tensor_scalar(u1[:], a_sb[:].indirect(first[:]), 1.0, 0.5, ALU.mult, ALU.add)
+        nc.vector.tensor_copy(a2[:], a_sb[:].indirect(second[:]))
+
+        last = len(CHUNKS) - 1
+        banks = []
+        for c, width in enumerate(CHUNKS):
+            grouped = sb.tile([P, width, PACK], BF16, name=f"v_grouped{c}", align_bytes=64)
+            share = SCALAR_SHARE[c]
+            interleave(nc.scalar.copy, grouped, v_raw[c], 0, share)
+            if share < width:
+                interleave(nc.vector.tensor_copy, grouped, v_raw[c], share, width)
+            codes, scales = quantize(grouped, f"v{c}", width)
+            acc = ps.tile([P, BANK], F32, name=f"c_bank{c}")
+            nc.tensor.matmul_mx(
+                out=acc[:, :width], lhsT=g_codes[:].bitcast(FP8X4), lhsT_scale=g_scales[:],
+                rhs=codes[:].bitcast(FP8X4), rhs_scale=scales[:], start=True, stop=True,
+            )
+            banks.append(acc)
+        c0_sb = sb.tile([P, T], F32, name=f"v_raw{last}")
+        for c, width in enumerate(CHUNKS):
+            nc.scalar.copy(c0_sb[:, STARTS[c] : STARTS[c] + width], banks[c][:, :width])
+
+        s = sb.tile([P, SLOTS], F32, name=f"v_grouped{last}", align_bytes=64)
+        neg_max = sb.tile([P, 1], F32, name="neg_max")
+        nc.vector.scalar_tensor_tensor(s[:], a2[:], 0.5, u1[:], ALU.add, ALU.mult)
+        nc.vector.tensor_reduce(neg_max[:], s[:], mybir.AxisListType.X, ALU.max, negate=True)
+        p = sb.tile([P, SLOTS], F32, name="p")
+        z = sb.tile([P, 1], F32, name="z")
+        nc.scalar.activation(p[:], s[:], ACT.Exp, bias=neg_max[:], scale=1.0, accum_out=z[:])
+
+        dw = sb.tile([P, SLOTS], F32, name="dw")
+        nc.vector.tensor_copy(dw[:], c0_sb[:].indirect(first[:]))
+        inv_z = sb.tile([P, 1], F32, name="inv_z")
+        nc.vector.reciprocal(inv_z[:], z[:])
+        f1 = sb.tile([P, SLOTS], F32, name="f1")
+        f2 = sb.tile([P, SLOTS], F32, name="f2")
+        coef = sb.tile([P, 2], F32, name="coef")
+        nc.scalar.activation(coef[:], consts[:], ACT.Copy, scale=inv_z[:])
+        nc.scalar.activation(f2[:], a2[:], ACT.Identity, scale=coef[:, 0:1], bias=coef[:, 1:2])
+        nc.scalar.activation(f1[:], u1[:], ACT.Copy, scale=coef[:, 0:1])
+        weighted = sb.tile([P, SLOTS], F32, name="weighted")
+        mean = sb.tile([P, 1], F32, name="mean")
+        nc.vector.scalar_tensor_tensor(weighted[:], dw[:], inv_z[:], p[:], ALU.mult, ALU.mult, accum_out=mean[:])
+        ds = sb.tile([P, SLOTS], F32, name="ds")
+        nc.vector.scalar_tensor_tensor(ds[:], dw[:], mean[:], p[:], ALU.subtract, ALU.mult)
+
+        nc.vector.tensor_tensor(by_first[:].indirect(first[:]), ds[:], f2[:], ALU.mult)
+        nc.vector.tensor_tensor(by_second[:].indirect(second[:]), ds[:], f1[:], ALU.mult)
+
+        blocks = BANK // P
+        turned = [ps.tile([P, BANK], F32, name=f"c_bank{last - half}") for half in range(2)]
+        for source, opens in ((old_sb, True), (by_first, False)):
+            for half in range(2):
+                for j in range(blocks):
+                    col = half * BANK + j * P
+                    nc.tensor.matmul(
+                        turned[half][:, j * P : (j + 1) * P], lhsT=source[:, col : col + P], rhs=ident[:],
+                        is_transpose=True, start=opens and j == 0, stop=not opens and j == blocks - 1,
+                    )
+        partial = []
+        for half in range(2):
+            turned_sb = sb.tile([P, BANK], F32, name=f"turned_sb{half}")
+            nc.scalar.copy(turned_sb[:], turned[half][:])
+            back = ps.tile([P, BANK], F32, name=f"a_bank{half}")
+            for j in range(blocks):
+                nc.tensor.transpose(back[:, j * P : (j + 1) * P], turned_sb[:, j * P : (j + 1) * P], ident[:])
+            partial.append(back)
+
+        width = T // PIECES
+        for piece in range(PIECES):
+            col = piece * width
+            result = sb.tile([P, width], F32, name=f"result{piece}")
+            nc.vector.tensor_tensor(
+                result[:], partial[col // BANK][:, col % BANK : col % BANK + width], by_second[:, col : col + width], ALU.add
+            )
+            queue = nc.sync if piece % 2 == 0 else nc.scalar
+            queue.dma_start(out=out[:, col : col + width], in_=result[:])

@@ -21,7 +21,7 @@ PACK = 4
 BANK = 512
 CHUNKS = (256, 256, 256, 256)
 STARTS = (0, 256, 512, 768)
-SCALAR_SHARE = (256, 256, 160, 96)
+SCALAR_SHARE = (256, 256, 160, 128)
 OUT_SCALE = 512.0
 PIECES = 4
 A_PARTS = 4
@@ -42,7 +42,8 @@ def tile_attend_bproductpairs_heads_kernel(tc, query, keys_words, keys_scales, g
 
         first = sb.tile([P, SLOTS // 16], U16, name="first")
         second = sb.tile([P, SLOTS // 16], U16, name="second")
-        k_codes = [sb.tile([P, BANK], U32, name=f"k_codes{h}", align_bytes=64) for h in range(2)]
+        k_all = sb.tile([P, T], U32, name="k_all", align_bytes=64)
+        k_codes = [k_all[:, :BANK], k_all[:, BANK:]]
         k_scales = sb.tile([P, T], U8, name="k_scales", align_bytes=64)
         q_raw = sb.tile([P, PACK, Q], F32, name="q_raw")
         g_raw = sb.tile([P, PACK, Q], F32, name="g_raw")
@@ -53,17 +54,16 @@ def tile_attend_bproductpairs_heads_kernel(tc, query, keys_words, keys_scales, g
         words = keys_words[0].rearrange("p n t -> p (n t)").bitcast(I32)
         vals_k = vals.rearrange("(p j) w -> p j w", j=PACK)
         nc.sync.dma_start(out=q_raw[:], in_=query.rearrange("(p j) w -> p j w", j=PACK))
-        nc.sync.dma_start(out=k_codes[0][:].bitcast(I32), in_=words[:, :BANK])
+        nc.sync.dma_start(first[:], offs)
+        nc.sync.dma_start(out=k_all[:].bitcast(I32), in_=words)
         for quad in range(4):
             nc.sync.dma_start(
                 out=k_scales[32 * quad : 32 * quad + 4, :].bitcast(I32),
                 in_=keys_scales[0, 4 * quad : 4 * quad + 4, :].bitcast(I32),
             )
-        nc.sync.dma_start(out=k_codes[1][:].bitcast(I32), in_=words[:, BANK:])
         nc.sync.dma_start(out=g_raw[:], in_=gout.rearrange("(p j) w -> p j w", j=PACK))
-        nc.sync.dma_start(first[:], offs)
-        nc.sync.dma_start(second[:], offs2)
         nc.sync.dma_start(out=v_raw[0][:], in_=vals_k[:, :, STARTS[0] : STARTS[0] + CHUNKS[0]])
+        nc.sync.dma_start(second[:], offs2)
         nc.sync.dma_start(out=v_raw[1][:], in_=vals_k[:, :, STARTS[1] : STARTS[1] + CHUNKS[1]])
         nc.sync.dma_start(out=v_raw[2][:], in_=vals_k[:, :, STARTS[2] : STARTS[2] + CHUNKS[2]])
         nc.sync.dma_start(out=v_raw[3][:], in_=vals_k[:, :, STARTS[3] : STARTS[3] + CHUNKS[3]])
@@ -74,9 +74,7 @@ def tile_attend_bproductpairs_heads_kernel(tc, query, keys_words, keys_scales, g
         nc.vector.memset(consts[:, 0:1], OUT_SCALE)
         nc.vector.memset(consts[:, 1:2], 0.5 * OUT_SCALE)
         by_first = sb.tile([P, T], F32, name="by_first")
-        by_second = sb.tile([P, T], F32, name="by_second")
         nc.vector.memset(by_first[:], 0.0)
-        nc.vector.memset(by_second[:], 0.0)
         ident = sb.tile([P, P], F32, name="ident")
         make_identity(nc, ident[:])
 
@@ -89,6 +87,8 @@ def tile_attend_bproductpairs_heads_kernel(tc, query, keys_words, keys_scales, g
         q_grouped = sb.tile([P, Q, PACK], BF16, name="q_grouped", align_bytes=64)
         interleave(nc.vector.tensor_copy, q_grouped, q_raw, 0, Q)
         q_codes, q_scales = quantize(q_grouped, "q", Q)
+        by_second = sb.tile([P, T], F32, name="q_grouped", align_bytes=64)
+        nc.vector.memset(by_second[:], 0.0)
 
         a_sb = sb.tile([P, T], F32, name="a_sb")
         a_width = T // A_PARTS

@@ -21,7 +21,7 @@ PACK = 4
 BANK = 512
 CHUNKS = (256, 256, 256, 256)
 STARTS = (0, 256, 512, 768)
-SCALAR_SHARE = (256, 256, 160, 128)
+SCALAR_SHARE = (256, 256, 192, 128)
 OUT_SCALE = 512.0
 PIECES = 4
 A_PARTS = 4
@@ -100,10 +100,7 @@ def tile_attend_bproductpairs_heads_kernel(tc, query, keys_words, keys_scales, g
                 rhs=k_codes[col // BANK][:, col % BANK : col % BANK + a_width].bitcast(FP8X4),
                 rhs_scale=k_scales[:, col : col + a_width], start=True, stop=True,
             )
-            if part % 2 == 0:
-                nc.scalar.activation(a_sb[:, col : col + a_width], acc[:, :a_width], ACT.Copy)
-            else:
-                nc.vector.tensor_copy(a_sb[:, col : col + a_width], acc[:, :a_width])
+            nc.scalar.activation(a_sb[:, col : col + a_width], acc[:, :a_width], ACT.Copy)
 
         g_grouped = sb.tile([P, Q, PACK], BF16, name="g_grouped", align_bytes=64)
         interleave(nc.vector.tensor_copy, g_grouped, g_raw, 0, Q)

from contextlib import ExitStack

import concourse.mybir as mybir
from concourse.masks import make_identity

D, E, T, Q, SLOTS = 512, 512, 1024, 128, 512
FLOPS = 2 * Q * T * (D + E)

F32 = mybir.dt.float32
BF16 = mybir.dt.bfloat16
I32 = mybir.dt.int32
U32 = mybir.dt.uint32
U16 = mybir.dt.uint16
U8 = mybir.dt.uint8
FP8X4 = mybir.dt.float8_e4m3fn_x4
ALU = mybir.AluOpType
ACT = mybir.ActivationFunctionType

P = 128
PACK = 4
BANK = 512
CHUNKS = (256, 256, 256, 256)
STARTS = (0, 256, 512, 768)
SCALAR_SHARE = (256, 256, 192, 128)
OUT_SCALE = 512.0
PIECES = 4
A_PARTS = 4


def interleave(copy, grouped, raw, c0, c1):
    copy(
        grouped[:, c0:c1, :].rearrange("p (c i) t -> p c t i", i=4),
        raw[:, :, c0:c1].rearrange("p t (c i) -> p c t i", i=4),
    )


def tile_attend_bproductpairs_heads_kernel(tc, query, keys_words, keys_scales, gout, vals, old, offs, offs2, out):
    nc = tc.nc
    with ExitStack() as ctx:
        sb = ctx.enter_context(tc.tile_pool(name="sb", bufs=1))
        ps = ctx.enter_context(tc.psum_pool(name="ps", bufs=1))

        first = sb.tile([P, SLOTS // 16], U16, name="first")
        second = sb.tile([P, SLOTS // 16], U16, name="second")
        k_all = sb.tile([P, T], U32, name="k_all", align_bytes=64)
        k_codes = [k_all[:, :BANK], k_all[:, BANK:]]
        k_scales = sb.tile([P, T], U8, name="k_scales", align_bytes=64)
        q_raw = sb.tile([P, PACK, Q], F32, name="q_raw")
        g_raw = sb.tile([P, PACK, Q], F32, name="g_raw")
        v_raw = [sb.tile([P, PACK, width], F32, name=f"v_raw{c}") for c, width in enumerate(CHUNKS)]
        old_sb = sb.tile([P, T], F32, name="old_sb")

        nc.gpsimd.memset(k_scales[:].bitcast(I32), 0)
        words = keys_words[0].rearrange("p n t -> p (n t)").bitcast(I32)
        vals_k = vals.rearrange("(p j) w -> p j w", j=PACK)
        nc.sync.dma_start(out=q_raw[:], in_=query.rearrange("(p j) w -> p j w", j=PACK))
        nc.sync.dma_start(first[:], offs)
        nc.sync.dma_start(out=k_all[:].bitcast(I32), in_=words)
        for quad in range(4):
            nc.sync.dma_start(
                out=k_scales[32 * quad : 32 * quad + 4, :].bitcast(I32),
                in_=keys_scales[0, 4 * quad : 4 * quad + 4, :].bitcast(I32),
            )
        nc.sync.dma_start(out=g_raw[:], in_=gout.rearrange("(p j) w -> p j w", j=PACK))
        nc.sync.dma_start(out=v_raw[0][:], in_=vals_k[:, :, STARTS[0] : STARTS[0] + CHUNKS[0]])
        nc.sync.dma_start(second[:], offs2)
        nc.sync.dma_start(out=v_raw[1][:], in_=vals_k[:, :, STARTS[1] : STARTS[1] + CHUNKS[1]])
        nc.sync.dma_start(out=v_raw[2][:], in_=vals_k[:, :, STARTS[2] : STARTS[2] + CHUNKS[2]])
        nc.sync.dma_start(out=v_raw[3][:], in_=vals_k[:, :, STARTS[3] : STARTS[3] + CHUNKS[3]])
        nc.sync.dma_start(out=old_sb[:], in_=old)


        consts = sb.tile([P, 2], F32, name="consts")
        nc.vector.memset(consts[:, 0:1], OUT_SCALE)
        nc.vector.memset(consts[:, 1:2], 0.5 * OUT_SCALE)
        by_first = sb.tile([P, T], F32, name="by_first")
        nc.vector.memset(by_first[:], 0.0)
        ident = sb.tile([P, P], F32, name="ident")
        make_identity(nc, ident[:])

        def quantize(grouped, name, width):
            codes = sb.tile([P, width], U32, name=name + "_codes", align_bytes=64)
            scales = sb.tile([P, width], U8, name=name + "_scales", align_bytes=64)
            nc.vector.quantize_mx(out=codes[:].bitcast(FP8X4), scales=scales[:], in_=grouped[:].rearrange("p w j -> p (w j)"))
            return codes, scales

        q_grouped = sb.tile([P, Q, PACK], BF16, name="q_grouped", align_bytes=64)
        interleave(nc.vector.tensor_copy, q_grouped, q_raw, 0, Q)
        q_codes, q_scales = quantize(q_grouped, "q", Q)
        by_second = sb.tile([P, T], F32, name="q_grouped", align_bytes=64)
        nc.vector.memset(by_second[:], 0.0)

        a_sb = sb.tile([P, T], F32, name="a_sb")
        a_width = T // A_PARTS
        for part in range(A_PARTS):
            col = part * a_width
            acc = ps.tile([P, BANK], F32, name=f"a_bank{part}")
            nc.tensor.matmul_mx(
                out=acc[:, :a_width], lhsT=q_codes[:].bitcast(FP8X4), lhsT_scale=q_scales[:],
                rhs=k_codes[col // BANK][:, col % BANK : col % BANK + a_width].bitcast(FP8X4),
                rhs_scale=k_scales[:, col : col + a_width], start=True, stop=True,
            )
            nc.scalar.activation(a_sb[:, col : col + a_width], acc[:, :a_width], ACT.Copy)

        g_grouped = sb.tile([P, Q, PACK], BF16, name="g_grouped", align_bytes=64)
        interleave(nc.vector.tensor_copy, g_grouped, g_raw, 0, Q)
        g_codes, g_scales = quantize(g_grouped, "g", Q)

        u1 = sb.tile([P, SLOTS], F32, name="u1")
        a2 = sb.tile([P, SLOTS], F32, name="a2")
        nc.vector.tensor_scalar(u1[:], a_sb[:].indirect(first[:]), 1.0, 0.5, ALU.mult, ALU.add)
        nc.vector.tensor_copy(a2[:], a_sb[:].indirect(second[:]))

        last = len(CHUNKS) - 1
        banks = []
        for c, width in enumerate(CHUNKS):
            grouped = sb.tile([P, width, PACK], BF16, name=f"v_grouped{c}", align_bytes=64)
            share = SCALAR_SHARE[c]
            interleave(nc.scalar.copy, grouped, v_raw[c], 0, share)
            if share < width:
                interleave(nc.vector.tensor_copy, grouped, v_raw[c], share, width)
            codes, scales = quantize(grouped, f"v{c}", width)
            acc = ps.tile([P, BANK], F32, name=f"c_bank{c}")
            nc.tensor.matmul_mx(
                out=acc[:, :width], lhsT=g_codes[:].bitcast(FP8X4), lhsT_scale=g_scales[:],
                rhs=codes[:].bitcast(FP8X4), rhs_scale=scales[:], start=True, stop=True,
            )
            banks.append(acc)
        c0_sb = sb.tile([P, T], F32, name=f"v_raw{last}")
        for c, width in enumerate(CHUNKS):
            nc.scalar.copy(c0_sb[:, STARTS[c] : STARTS[c] + width], banks[c][:, :width])

        s = sb.tile([P, SLOTS], F32, name=f"v_grouped{last}", align_bytes=64)
        neg_max = sb.tile([P, 1], F32, name="neg_max")
        nc.vector.scalar_tensor_tensor(s[:], a2[:], 0.5, u1[:], ALU.add, ALU.mult)
        nc.vector.tensor_reduce(neg_max[:], s[:], mybir.AxisListType.X, ALU.max, negate=True)
        p = sb.tile([P, SLOTS], F32, name="p")
        z = sb.tile([P, 1], F32, name="z")
        nc.scalar.activation(p[:], s[:], ACT.Exp, bias=neg_max[:], scale=1.0, accum_out=z[:])

        dw = sb.tile([P, SLOTS], F32, name="dw")
        nc.vector.tensor_copy(dw[:], c0_sb[:].indirect(first[:]))
        inv_z = sb.tile([P, 1], F32, name="inv_z")
        nc.vector.reciprocal(inv_z[:], z[:])
        f1 = sb.tile([P, SLOTS], F32, name="f1")
        f2 = sb.tile([P, SLOTS], F32, name="f2")
        coef = sb.tile([P, 2], F32, name="coef")
        nc.scalar.activation(coef[:], consts[:], ACT.Copy, scale=inv_z[:])
        nc.scalar.activation(f2[:], a2[:], ACT.Identity, scale=coef[:, 0:1], bias=coef[:, 1:2])
        nc.scalar.activation(f1[:], u1[:], ACT.Copy, scale=coef[:, 0:1])
        weighted = sb.tile([P, SLOTS], F32, name="weighted")
        mean = sb.tile([P, 1], F32, name="mean")
        nc.vector.scalar_tensor_tensor(weighted[:], dw[:], inv_z[:], p[:], ALU.mult, ALU.mult, accum_out=mean[:])
        ds = sb.tile([P, SLOTS], F32, name="ds")
        nc.vector.scalar_tensor_tensor(ds[:], dw[:], mean[:], p[:], ALU.subtract, ALU.mult)

        nc.vector.tensor_tensor(by_first[:].indirect(first[:]), ds[:], f2[:], ALU.mult)
        nc.vector.tensor_tensor(by_second[:].indirect(second[:]), ds[:], f1[:], ALU.mult)

        blocks = BANK // P
        turned = [ps.tile([P, BANK], F32, name=f"c_bank{last - half}") for half in range(2)]
        for source, opens in ((old_sb, True), (by_first, False)):
            for half in range(2):
                for j in range(blocks):
                    col = half * BANK + j * P
                    nc.tensor.matmul(
                        turned[half][:, j * P : (j + 1) * P], lhsT=source[:, col : col + P], rhs=ident[:],
                        is_transpose=True, start=opens and j == 0, stop=not opens and j == blocks - 1,
                    )
        partial = []
        for half in range(2):
            turned_sb = sb.tile([P, BANK], F32, name=f"turned_sb{half}")
            nc.scalar.copy(turned_sb[:], turned[half][:])
            back = ps.tile([P, BANK], F32, name=f"a_bank{half}")
            for j in range(blocks):
                nc.tensor.transpose(back[:, j * P : (j + 1) * P], turned_sb[:, j * P : (j + 1) * P], ident[:])
            partial.append(back)

        width = T // PIECES
        for piece in range(PIECES):
            col = piece * width
            result = sb.tile([P, width], F32, name=f"result{piece}")
            nc.vector.tensor_tensor(
                result[:], partial[col // BANK][:, col % BANK : col % BANK + width], by_second[:, col : col + width], ALU.add
            )
            queue = nc.sync if piece % 2 == 0 else nc.scalar
            queue.dma_start(out=out[:, col : col + width], in_=result[:])
